import numpy as np
import ml_dtypes


def mxq(x, axis, fmt="e4m3"):
    dtype, down = {"e4m3": (ml_dtypes.float8_e4m3fn, 7), "e5m2": (ml_dtypes.float8_e5m2, 14)}[fmt]
    v = np.moveaxis(np.asarray(x, np.float32).astype(ml_dtypes.bfloat16).astype(np.float64), axis, -1)
    blocks = v.reshape(v.shape[:-1] + (-1, 32))
    amax = np.abs(blocks).max(-1, keepdims=True)
    byte = np.maximum(np.where(amax > 0, np.frexp(amax)[1] - 1 + 127, 0) - down, 1)
    scale = np.exp2(byte - 127.0)
    codes = (blocks / scale).astype(np.float32).astype(dtype).astype(np.float64)
    return np.moveaxis((codes * scale).reshape(v.shape), -1, axis)


WIDE = False


def mx_kscale(k):
    if not WIDE:
        return np.ones(k)
    levels = np.array([10, -10, 5, -5, 0])
    if k % 512:
        return np.exp2(np.random.permutation(np.resize(levels, k // 32))).repeat(32)
    a = np.empty((k // 512, 16))
    for p in range(k // 512):
        a[p, :8] = np.random.permutation(np.resize(levels, 8))
        for g in range(8):
            far = levels[np.abs(levels - a[p, g]) >= 10]
            a[p, g + 8] = far[np.random.randint(len(far))]
    return np.exp2(a.ravel()).repeat(32)


def f64(x):
    return np.asarray(x).astype(np.float64)


def striped(idx):
    return np.tile(np.asarray(idx).reshape(-1, 16).T, (8, 1)).astype(np.uint16)


def unstriped(offs):
    return offs[:16].T.reshape(-1).astype(np.int64)


E2M1 = np.array([0.0, 0.5, 1.0, 1.5, 2.0, 3.0, 4.0, 6.0, -0.0, -0.5, -1.0, -1.5, -2.0, -3.0, -4.0, -6.0])


def pack_weight(w, fmt):
    k, n = w.shape
    w = f64(np.asarray(w, np.float32).astype(ml_dtypes.bfloat16)).reshape(k // 32, 32, n)
    amax = np.abs(w).max(1)
    if fmt == "e4m3":
        byte = np.frexp(amax)[1] - 1 + 127 - 7
    else:
        mant, ex = np.frexp(amax / 6.0)
        byte = np.where(mant > 0.5, ex, ex - 1) + 127
    byte = np.clip(np.where(amax > 0, byte, 1), 1, 254)
    scaled = (w * np.exp2(127.0 - byte)[:, None, :]).reshape(k, n).astype(np.float32)
    by_word = np.ascontiguousarray(scaled.reshape(k // 512, 128, 4, n).transpose(0, 1, 3, 2))
    if fmt == "e4m3":
        words = by_word.astype(ml_dtypes.float8_e4m3fn).view(np.uint8)
    else:
        c = by_word.astype(ml_dtypes.float4_e2m1fn).view(np.uint8) & 0xF
        words = (c[..., 0::2] | (c[..., 1::2] << 4)).reshape(k // 512, 128, 2 * n)
    return np.ascontiguousarray(words), np.ascontiguousarray(byte.astype(np.uint8).reshape(k // 512, 16, n))


def unpack_weight(words, scales, fmt):
    g, _, n = scales.shape
    words = np.ascontiguousarray(words).reshape(g, 128, n, -1)
    if fmt == "e4m3":
        vals = words.view(ml_dtypes.float8_e4m3fn).astype(np.float64)
    else:
        nib = np.empty((g, 128, n, 4), np.uint8)
        nib[..., 0::2] = words & 0xF
        nib[..., 1::2] = words >> 4
        vals = E2M1[nib]
    vals = vals * np.repeat(np.exp2(scales.astype(np.float64) - 127.0), 8, axis=1)[..., None]
    return vals.transpose(0, 1, 3, 2).reshape(g * 512, n)


D, T, I, Q, J, M = 512, 2048, 512, 128, 512, 2048


def setup_inputs():
    n = np.random.standard_normal
    idx = np.random.permutation(T)[:I]
    idx2 = np.random.permutation(T)[:J]
    idx3 = np.random.permutation(M)[:I]
    fd = mx_kscale(D)
    fj = mx_kscale(J)
    keysp = pack_weight(n((D, T)) / fd[:, None], "e4m3")
    return {
        "query": (n((D, Q)) * 0.39 / np.sqrt(D) * fd[:, None]).astype(np.float32),
        "keys_words": keysp[0],
        "keys_scales": keysp[1],
        "hf": (np.random.uniform(0.5, 2.0, (J, 1)) * fj[:, None]).astype(np.float32),
        "mixer": (n((J, I)) * 0.05 / fj[:, None]).astype(np.float32),
        "pull": (np.random.uniform(0.3, 0.9, (Q, 1))).astype(np.float32),
        "old": (np.random.uniform(0.0, 2.0, (Q, M))).astype(np.float32),
        "fade": (np.random.uniform(0.3, 0.9, (Q, 1))).astype(np.float32),
        "offs": striped(idx),
        "offs2": striped(idx2),
        "offs3": striped(idx3),
    }


def reference(query, keys_words, keys_scales, hf, mixer, pull, old, fade, offs, offs2, offs3):
    idx = unstriped(offs)
    idx2 = unstriped(offs2)
    idx3 = unstriped(offs3)
    keysu = unpack_weight(keys_words, keys_scales, "e4m3")
    keysidx2g = keysu[:, idx2]
    queryq = mxq(f64(query), 0, "e4m3")
    a0 = keysidx2g.T @ queryq
    af = a0 * f64(hf)
    afq = mxq(af, 0, "e4m3")
    mixerq = mxq(f64(mixer), 0, "e4m3")
    mx0 = afq.T @ mixerq
    keysidxg = keysu[:, idx]
    a = queryq.T @ keysidxg
    s = a + mx0
    p = np.exp(s - np.max(s, axis=1, keepdims=True))
    r = p / np.sum(p, axis=1, keepdims=True)
    r1 = np.pad(r, ((0, 0), (1, 0)))[:, :I]
    w = r - r1 * f64(pull)
    ws = w * 256.0
    wf = np.zeros((Q, M))
    wf[:, idx3] = ws
    y = f64(old) * f64(fade) + wf
    return y

@@ -1,0 +1,193 @@
+from contextlib import ExitStack
+
+import concourse.mybir as mybir
+
+D, T, I, Q, J, M = 512, 2048, 512, 128, 512, 2048
+FLOPS = 2 * D * J * Q + 2 * J * I * Q + 2 * D * I * Q
+
+F32 = mybir.dt.float32
+BF16 = mybir.dt.bfloat16
+I32 = mybir.dt.int32
+U32 = mybir.dt.uint32
+U16 = mybir.dt.uint16
+U8 = mybir.dt.uint8
+FP8X4 = mybir.dt.float8_e4m3fn_x4
+ALU = mybir.AluOpType
+ACT = mybir.ActivationFunctionType
+AX = mybir.AxisListType
+
+P = 128
+PACK = 4
+RUN = 4
+GAIN = 256.0
+PAD = 8
+MIXER_WIDTHS = (256, 128, 128)
+OUT_WIDTHS = (256, 512, 512, 512, 256)
+
+
+def interleave_cast(nc, grouped, raw):
+    nc.scalar.copy(
+        out=grouped.rearrange("p (c i) t -> p c t i", i=RUN),
+        in_=raw.rearrange("p t (c i) -> p c t i", i=RUN),
+    )
+
+
+def tile_attend_mixedslots_stepwise_counts_kernel(
+    tc, query, keys_words, keys_scales, hf, mixer, pull, old, fade, offs, offs2, offs3, out
+):
+    nc = tc.nc
+    with ExitStack() as ctx:
+        lists = ctx.enter_context(tc.tile_pool(name="lists", bufs=1))
+        sb = ctx.enter_context(tc.tile_pool(name="sb", bufs=1))
+        psum = ctx.enter_context(tc.psum_pool(name="psum", bufs=1))
+
+        offs_t = lists.tile([P, I // 16], U16, name="offs_t")
+        offs2_t = lists.tile([P, J // 16], U16, name="offs2_t")
+        offs3_t = lists.tile([P, I // 16], U16, name="offs3_t")
+
+        pool_scales = sb.tile([P, T], U8, name="pool_scales", align_bytes=64)
+        pool_words = sb.tile([P, T], I32, name="pool_words", align_bytes=64)
+        q_raw = sb.tile([P, PACK, Q], F32, name="q_raw", align_bytes=64)
+        placed = sb.tile([P, M], F32, name="placed", align_bytes=64)
+        p_pad = sb.tile([P, PAD + I], F32, name="p_pad", align_bytes=64)
+        old_t = sb.tile([P, M], F32, name="old_t", align_bytes=64)
+        hf_t = sb.tile([P, PACK], F32, name="hf_t")
+        pull_t = sb.tile([P, 1], F32, name="pull_t")
+        fade_t = sb.tile([P, 1], F32, name="fade_t")
+
+        nc.vector.memset(pool_scales[:].bitcast(I32), 0)
+
+        nc.sync.dma_start(out=offs2_t[:], in_=offs2)
+        nc.sync.dma_start(out=q_raw[:], in_=query.rearrange("(p t) q -> p t q", t=PACK))
+        nc.sync.dma_start(out=offs_t[:], in_=offs)
+        for quad in range(4):
+            nc.sync.dma_start(
+                out=pool_scales[32 * quad : 32 * quad + 4, :].bitcast(I32),
+                in_=keys_scales[0, 4 * quad : 4 * quad + 4, :].bitcast(I32),
+            )
+        nc.sync.dma_start(out=pool_words[:], in_=keys_words[0].rearrange("p n t -> p (n t)").bitcast(I32))
+        nc.sync.dma_start(out=hf_t[:], in_=hf.rearrange("(p t) o -> p (t o)", t=PACK))
+        mixer_rows = mixer.rearrange("(p t) i -> p t i", t=PACK)
+        mixer_raw = []
+        col = 0
+        for c, width in enumerate(MIXER_WIDTHS):
+            raw = sb.tile([P, PACK, width], F32, name=f"mixer_raw{c}", align_bytes=64)
+            nc.sync.dma_start(out=raw[:], in_=mixer_rows[:, :, col : col + width])
+            mixer_raw.append((raw, col, width))
+            col = col + width
+        nc.sync.dma_start(out=offs3_t[:], in_=offs3)
+        nc.sync.dma_start(out=pull_t[:], in_=pull)
+        nc.sync.dma_start(out=fade_t[:], in_=fade)
+        nc.sync.dma_start(out=old_t[:], in_=old)
+
+        nc.vector.memset(placed[:], 0.0)
+        nc.vector.memset(p_pad[:, PAD - 1 : PAD], 0.0)
+        pull_gain = sb.tile([P, 1], F32, name="pull_gain")
+        nc.gpsimd.tensor_scalar(pull_gain[:], pull_t[:], -GAIN, 0.0, ALU.mult, ALU.add)
+
+        mixed_scales = sb.tile([P, J], U8, name="mixed_scales", align_bytes=64)
+        mixed_words = sb.tile([P, J], U32, name="mixed_words", align_bytes=64)
+        own_scales = sb.tile([P, I], U8, name="own_scales", align_bytes=64)
+        own_words = sb.tile([P, I], U32, name="own_words", align_bytes=64)
+        words_window = pool_words[:].bitcast(U32)
+
+        nc.vector.tensor_copy(
+            out=mixed_scales[:].rearrange("p (r s) -> p s r", r=PACK), in_=pool_scales[:].indirect(offs2_t[:])
+        )
+        nc.vector.tensor_copy(out=own_scales[:], in_=pool_scales[:].indirect(offs_t[:]))
+
+        q_bf = sb.tile([P, Q, PACK], BF16, name="q_bf", align_bytes=64)
+        q_codes = sb.tile([P, Q], U32, name="q_codes", align_bytes=64)
+        q_scales = sb.tile([P, Q], U8, name="q_scales", align_bytes=64)
+        interleave_cast(nc, q_bf[:], q_raw[:])
+        nc.vector.quantize_mx(
+            out=q_codes[:].bitcast(FP8X4), scales=q_scales[:], in_=q_bf[:].rearrange("p q t -> p (q t)")
+        )
+
+        nc.vector.tensor_copy(
+            out=mixed_words[:].rearrange("p (r s) -> p s r", r=PACK), in_=words_window.indirect(offs2_t[:])
+        )
+        a0 = psum.tile([P, PACK, Q], F32, name="a0")
+        for r in range(PACK):
+            cols = slice(r * P, (r + 1) * P)
+            nc.tensor.matmul_mx(
+                out=a0[:, r, :],
+                lhsT=mixed_words[:, cols].bitcast(FP8X4),
+                lhsT_scale=mixed_scales[:, cols],
+                rhs=q_codes[:].bitcast(FP8X4),
+                rhs_scale=q_scales[:],
+                start=True,
+                stop=True,
+            )
+
+        nc.vector.tensor_copy(out=own_words[:], in_=words_window.indirect(offs_t[:]))
+        scores = psum.tile([P, I], F32, name="scores")
+        nc.tensor.matmul_mx(
+            out=scores[:],
+            lhsT=q_codes[:].bitcast(FP8X4),
+            lhsT_scale=q_scales[:],
+            rhs=own_words[:].bitcast(FP8X4),
+            rhs_scale=own_scales[:],
+            start=True,
+            stop=False,
+        )
+
+        af_bf = sb.tile([P, Q, PACK], BF16, name="af_bf", align_bytes=64)
+        nc.vector.tensor_tensor(
+            out=af_bf[:],
+            in0=a0[:].rearrange("p r q -> p q r"),
+            in1=hf_t[:].unsqueeze(1).to_broadcast([P, Q, PACK]),
+            op=ALU.mult,
+        )
+
+        mixer_codes = sb.tile([P, I], U32, name="mixer_codes", align_bytes=64)
+        mixer_scales = sb.tile([P, I], U8, name="mixer_scales", align_bytes=64)
+        for c, (raw, col, width) in enumerate(mixer_raw):
+            grouped = sb.tile([P, width, PACK], BF16, name=f"mixer_bf{c}", align_bytes=64)
+            interleave_cast(nc, grouped[:], raw[:])
+            nc.vector.quantize_mx(
+                out=mixer_codes[:, col : col + width].bitcast(FP8X4),
+                scales=mixer_scales[:, col : col + width],
+                in_=grouped[:].rearrange("p i t -> p (i t)"),
+            )
+
+        af_codes = sb.tile([P, Q], U32, name="af_codes", align_bytes=64)
+        af_scales = sb.tile([P, Q], U8, name="af_scales", align_bytes=64)
+        nc.vector.quantize_mx(
+            out=af_codes[:].bitcast(FP8X4), scales=af_scales[:], in_=af_bf[:].rearrange("p q t -> p (q t)")
+        )
+        nc.tensor.matmul_mx(
+            out=scores[:],
+            lhsT=af_codes[:].bitcast(FP8X4),
+            lhsT_scale=af_scales[:],
+            rhs=mixer_codes[:].bitcast(FP8X4),
+            rhs_scale=mixer_scales[:],
+            start=False,
+            stop=True,
+        )
+
+        neg_max = sb.tile([P, 1], F32, name="neg_max")
+        row_sum = sb.tile([P, 1], F32, name="row_sum")
+        inv_sum = sb.tile([P, 1], F32, name="inv_sum")
+        nc.vector.tensor_reduce(out=neg_max[:], in_=scores[:], axis=AX.X, op=ALU.max, negate=True)
+        nc.scalar.activation(
+            out=p_pad[:, PAD : PAD + I], in_=scores[:], func=ACT.Exp, bias=neg_max[:], accum_out=row_sum[:]
+        )
+        nc.vector.reciprocal(out=inv_sum[:], in_=row_sum[:])
+        share = sb.tile([P, I], F32, name="share", align_bytes=64)
+        pulled = sb.tile([P, I], F32, name="pulled", align_bytes=64)
+        nc.vector.tensor_scalar(share[:], p_pad[:, PAD : PAD + I], inv_sum[:], GAIN, ALU.mult, ALU.mult)
+        nc.vector.tensor_scalar(
+            pulled[:], p_pad[:, PAD - 1 : PAD - 1 + I], inv_sum[:], pull_gain[:], ALU.mult, ALU.mult
+        )
+        nc.vector.tensor_tensor(out=placed[:].indirect(offs3_t[:]), in0=share[:], in1=pulled[:], op=ALU.add)
+
+        col = 0
+        for c, width in enumerate(OUT_WIDTHS):
+            cols = slice(col, col + width)
+            result = sb.tile([P, width], F32, name=f"result{c}", align_bytes=64)
+            nc.vector.scalar_tensor_tensor(
+                out=result[:], in0=old_t[:, cols], scalar=fade_t[:], in1=placed[:, cols], op0=ALU.mult, op1=ALU.add
+            )
+            nc.sync.dma_start(out=out[:, cols], in_=result[:])
+            col = col + width

@@ -22,7 +22,9 @@ RUN = 4
 GAIN = 256.0
 PAD = 8
 MIXER_WIDTHS = (256, 128, 128)
-OUT_WIDTHS = (256, 512, 512, 512, 256)
+SCALAR_SLOTS = 384
+OUT_WIDTH = 256
+EARLY_CHUNKS = 6
 
 
 def interleave_cast(nc, grouped, raw):
@@ -48,7 +50,8 @@ def tile_attend_mixedslots_stepwise_counts_kernel(
         pool_scales = sb.tile([P, T], U8, name="pool_scales", align_bytes=64)
         pool_words = sb.tile([P, T], I32, name="pool_words", align_bytes=64)
         q_raw = sb.tile([P, PACK, Q], F32, name="q_raw", align_bytes=64)
-        placed = sb.tile([P, M], F32, name="placed", align_bytes=64)
+        placed_v = sb.tile([P, M], F32, name="placed_v", align_bytes=64)
+        placed_s = sb.tile([P, M], F32, name="placed_s", align_bytes=64)
         p_pad = sb.tile([P, PAD + I], F32, name="p_pad", align_bytes=64)
         old_t = sb.tile([P, M], F32, name="old_t", align_bytes=64)
         hf_t = sb.tile([P, PACK], F32, name="hf_t")
@@ -80,9 +83,12 @@ def tile_attend_mixedslots_stepwise_counts_kernel(
         nc.sync.dma_start(out=fade_t[:], in_=fade)
         nc.sync.dma_start(out=old_t[:], in_=old)
 
-        nc.vector.memset(placed[:], 0.0)
+        nc.vector.memset(placed_s[:], 0.0)
+        nc.vector.memset(placed_v[:], 0.0)
         nc.vector.memset(p_pad[:, PAD - 1 : PAD], 0.0)
         pull_gain = sb.tile([P, 1], F32, name="pull_gain")
+        neg_pull = sb.tile([P, 1], F32, name="neg_pull")
+        nc.gpsimd.tensor_scalar(neg_pull[:], pull_t[:], -1.0, 0.0, ALU.mult, ALU.add)
         nc.gpsimd.tensor_scalar(pull_gain[:], pull_t[:], -GAIN, 0.0, ALU.mult, ALU.add)
 
         mixed_scales = sb.tile([P, J], U8, name="mixed_scales", align_bytes=64)
@@ -142,29 +148,30 @@ def tile_attend_mixedslots_stepwise_counts_kernel(
 
         mixer_codes = sb.tile([P, I], U32, name="mixer_codes", align_bytes=64)
         mixer_scales = sb.tile([P, I], U8, name="mixer_scales", align_bytes=64)
+        af_codes = sb.tile([P, Q], U32, name="af_codes", align_bytes=64)
+        af_scales = sb.tile([P, Q], U8, name="af_scales", align_bytes=64)
         for c, (raw, col, width) in enumerate(mixer_raw):
+            cols = slice(col, col + width)
             grouped = sb.tile([P, width, PACK], BF16, name=f"mixer_bf{c}", align_bytes=64)
             interleave_cast(nc, grouped[:], raw[:])
             nc.vector.quantize_mx(
-                out=mixer_codes[:, col : col + width].bitcast(FP8X4),
-                scales=mixer_scales[:, col : col + width],
+                out=mixer_codes[:, cols].bitcast(FP8X4),
+                scales=mixer_scales[:, cols],
                 in_=grouped[:].rearrange("p i t -> p (i t)"),
             )
-
-        af_codes = sb.tile([P, Q], U32, name="af_codes", align_bytes=64)
-        af_scales = sb.tile([P, Q], U8, name="af_scales", align_bytes=64)
-        nc.vector.quantize_mx(
-            out=af_codes[:].bitcast(FP8X4), scales=af_scales[:], in_=af_bf[:].rearrange("p q t -> p (q t)")
-        )
-        nc.tensor.matmul_mx(
-            out=scores[:],
-            lhsT=af_codes[:].bitcast(FP8X4),
-            lhsT_scale=af_scales[:],
-            rhs=mixer_codes[:].bitcast(FP8X4),
-            rhs_scale=mixer_scales[:],
-            start=False,
-            stop=True,
-        )
+            if c == 0:
+                nc.vector.quantize_mx(
+                    out=af_codes[:].bitcast(FP8X4), scales=af_scales[:], in_=af_bf[:].rearrange("p q t -> p (q t)")
+                )
+            nc.tensor.matmul_mx(
+                out=scores[:, cols],
+                lhsT=af_codes[:].bitcast(FP8X4),
+                lhsT_scale=af_scales[:],
+                rhs=mixer_codes[:, cols].bitcast(FP8X4),
+                rhs_scale=mixer_scales[:, cols],
+                start=False,
+                stop=(c == len(mixer_raw) - 1),
+            )
 
         neg_max = sb.tile([P, 1], F32, name="neg_max")
         row_sum = sb.tile([P, 1], F32, name="row_sum")
@@ -174,20 +181,50 @@ def tile_attend_mixedslots_stepwise_counts_kernel(
             out=p_pad[:, PAD : PAD + I], in_=scores[:], func=ACT.Exp, bias=neg_max[:], accum_out=row_sum[:]
         )
         nc.vector.reciprocal(out=inv_sum[:], in_=row_sum[:])
-        share = sb.tile([P, I], F32, name="share", align_bytes=64)
-        pulled = sb.tile([P, I], F32, name="pulled", align_bytes=64)
-        nc.vector.tensor_scalar(share[:], p_pad[:, PAD : PAD + I], inv_sum[:], GAIN, ALU.mult, ALU.mult)
-        nc.vector.tensor_scalar(
-            pulled[:], p_pad[:, PAD - 1 : PAD - 1 + I], inv_sum[:], pull_gain[:], ALU.mult, ALU.mult
+        rest = I - SCALAR_SLOTS
+        step_s = sb.tile([P, SCALAR_SLOTS], F32, name="step_s", align_bytes=64)
+        ws_s = sb.tile([P, SCALAR_SLOTS], F32, name="ws_s", align_bytes=64)
+        share = sb.tile([P, rest], F32, name="share", align_bytes=64)
+        pulled = sb.tile([P, rest], F32, name="pulled", align_bytes=64)
+        nc.vector.scalar_tensor_tensor(
+            out=step_s[:],
+            in0=p_pad[:, PAD - 1 : PAD - 1 + SCALAR_SLOTS],
+            scalar=neg_pull[:],
+            in1=p_pad[:, PAD : PAD + SCALAR_SLOTS],
+            op0=ALU.mult,
+            op1=ALU.add,
         )
-        nc.vector.tensor_tensor(out=placed[:].indirect(offs3_t[:]), in0=share[:], in1=pulled[:], op=ALU.add)
+        first = PAD + SCALAR_SLOTS
+        nc.vector.tensor_scalar(share[:], p_pad[:, first : first + rest], inv_sum[:], GAIN, ALU.mult, ALU.mult)
+        nc.vector.tensor_scalar(
+            pulled[:], p_pad[:, first - 1 : first - 1 + rest], inv_sum[:], pull_gain[:], ALU.mult, ALU.mult
+        )
+        nc.vector.tensor_scalar(ws_s[:], step_s[:], inv_sum[:], GAIN, ALU.mult, ALU.mult)
+        nc.scalar.activation(
+            out=placed_s[:].indirect(offs3_t[:, : SCALAR_SLOTS // 16]), in_=ws_s[:], func=ACT.Copy
+        )
+        nc.vector.tensor_tensor(
+            out=placed_v[:].indirect(offs3_t[:, SCALAR_SLOTS // 16 :]), in0=share[:], in1=pulled[:], op=ALU.add
+        )
 
-        col = 0
-        for c, width in enumerate(OUT_WIDTHS):
-            cols = slice(col, col + width)
-            result = sb.tile([P, width], F32, name=f"result{c}", align_bytes=64)
+        partial = sb.tile([P, M], F32, name="partial", align_bytes=64)
+
+        def fade_and_add(cols):
             nc.vector.scalar_tensor_tensor(
-                out=result[:], in0=old_t[:, cols], scalar=fade_t[:], in1=placed[:, cols], op0=ALU.mult, op1=ALU.add
+                out=partial[:, cols],
+                in0=old_t[:, cols],
+                scalar=fade_t[:],
+                in1=placed_v[:, cols],
+                op0=ALU.mult,
+                op1=ALU.add,
             )
+
+        chunks = M // OUT_WIDTH
+        fade_and_add(slice(0, EARLY_CHUNKS * OUT_WIDTH))
+        for c in range(chunks):
+            if EARLY_CHUNKS <= c + 1 < chunks:
+                fade_and_add(slice((c + 1) * OUT_WIDTH, (c + 2) * OUT_WIDTH))
+            cols = slice(c * OUT_WIDTH, (c + 1) * OUT_WIDTH)
+            result = sb.tile([P, OUT_WIDTH], F32, name=f"result{c}", align_bytes=64)
+            nc.vector.tensor_tensor(out=result[:], in0=partial[:, cols], in1=placed_s[:, cols], op=ALU.add)
             nc.sync.dma_start(out=out[:, cols], in_=result[:])
-            col = col + width

from contextlib import ExitStack

import concourse.mybir as mybir

D, T, I, Q, J, M = 512, 2048, 512, 128, 512, 2048
FLOPS = 2 * D * J * Q + 2 * J * I * Q + 2 * D * I * Q

F32 = mybir.dt.float32
BF16 = mybir.dt.bfloat16
I32 = mybir.dt.int32
U32 = mybir.dt.uint32
U16 = mybir.dt.uint16
U8 = mybir.dt.uint8
FP8X4 = mybir.dt.float8_e4m3fn_x4
ALU = mybir.AluOpType
ACT = mybir.ActivationFunctionType
AX = mybir.AxisListType

P = 128
PACK = 4
RUN = 4
GAIN = 256.0
PAD = 8
MIXER_WIDTHS = (256, 128, 128)
SCALAR_SLOTS = 384
OUT_WIDTH = 256
EARLY_CHUNKS = 6


def interleave_cast(nc, grouped, raw):
    nc.scalar.copy(
        out=grouped.rearrange("p (c i) t -> p c t i", i=RUN),
        in_=raw.rearrange("p t (c i) -> p c t i", i=RUN),
    )


def tile_attend_mixedslots_stepwise_counts_kernel(
    tc, query, keys_words, keys_scales, hf, mixer, pull, old, fade, offs, offs2, offs3, out
):
    nc = tc.nc
    with ExitStack() as ctx:
        lists = ctx.enter_context(tc.tile_pool(name="lists", bufs=1))
        sb = ctx.enter_context(tc.tile_pool(name="sb", bufs=1))
        psum = ctx.enter_context(tc.psum_pool(name="psum", bufs=1))

        offs_t = lists.tile([P, I // 16], U16, name="offs_t")
        offs2_t = lists.tile([P, J // 16], U16, name="offs2_t")
        offs3_t = lists.tile([P, I // 16], U16, name="offs3_t")

        pool_scales = sb.tile([P, T], U8, name="pool_scales", align_bytes=64)
        pool_words = sb.tile([P, T], I32, name="pool_words", align_bytes=64)
        q_raw = sb.tile([P, PACK, Q], F32, name="q_raw", align_bytes=64)
        placed_v = sb.tile([P, M], F32, name="placed_v", align_bytes=64)
        placed_s = sb.tile([P, M], F32, name="placed_s", align_bytes=64)
        p_pad = sb.tile([P, PAD + I], F32, name="p_pad", align_bytes=64)
        old_t = sb.tile([P, M], F32, name="old_t", align_bytes=64)
        hf_t = sb.tile([P, PACK], F32, name="hf_t")
        pull_t = sb.tile([P, 1], F32, name="pull_t")
        fade_t = sb.tile([P, 1], F32, name="fade_t")

        nc.vector.memset(pool_scales[:].bitcast(I32), 0)

        nc.sync.dma_start(out=offs2_t[:], in_=offs2)
        nc.sync.dma_start(out=q_raw[:], in_=query.rearrange("(p t) q -> p t q", t=PACK))
        nc.sync.dma_start(out=offs_t[:], in_=offs)
        for quad in range(4):
            nc.sync.dma_start(
                out=pool_scales[32 * quad : 32 * quad + 4, :].bitcast(I32),
                in_=keys_scales[0, 4 * quad : 4 * quad + 4, :].bitcast(I32),
            )
        nc.sync.dma_start(out=pool_words[:], in_=keys_words[0].rearrange("p n t -> p (n t)").bitcast(I32))
        nc.sync.dma_start(out=hf_t[:], in_=hf.rearrange("(p t) o -> p (t o)", t=PACK))
        mixer_rows = mixer.rearrange("(p t) i -> p t i", t=PACK)
        mixer_raw = []
        col = 0
        for c, width in enumerate(MIXER_WIDTHS):
            raw = sb.tile([P, PACK, width], F32, name=f"mixer_raw{c}", align_bytes=64)
            nc.sync.dma_start(out=raw[:], in_=mixer_rows[:, :, col : col + width])
            mixer_raw.append((raw, col, width))
            col = col + width
        nc.sync.dma_start(out=offs3_t[:], in_=offs3)
        nc.sync.dma_start(out=pull_t[:], in_=pull)
        nc.sync.dma_start(out=fade_t[:], in_=fade)
        nc.sync.dma_start(out=old_t[:], in_=old)

        nc.vector.memset(placed_s[:], 0.0)
        nc.vector.memset(placed_v[:], 0.0)
        nc.vector.memset(p_pad[:, PAD - 1 : PAD], 0.0)
        pull_gain = sb.tile([P, 1], F32, name="pull_gain")
        neg_pull = sb.tile([P, 1], F32, name="neg_pull")
        nc.gpsimd.tensor_scalar(neg_pull[:], pull_t[:], -1.0, 0.0, ALU.mult, ALU.add)
        nc.gpsimd.tensor_scalar(pull_gain[:], pull_t[:], -GAIN, 0.0, ALU.mult, ALU.add)

        mixed_scales = sb.tile([P, J], U8, name="mixed_scales", align_bytes=64)
        mixed_words = sb.tile([P, J], U32, name="mixed_words", align_bytes=64)
        own_scales = sb.tile([P, I], U8, name="own_scales", align_bytes=64)
        own_words = sb.tile([P, I], U32, name="own_words", align_bytes=64)
        words_window = pool_words[:].bitcast(U32)

        nc.vector.tensor_copy(
            out=mixed_scales[:].rearrange("p (r s) -> p s r", r=PACK), in_=pool_scales[:].indirect(offs2_t[:])
        )
        nc.vector.tensor_copy(out=own_scales[:], in_=pool_scales[:].indirect(offs_t[:]))

        q_bf = sb.tile([P, Q, PACK], BF16, name="q_bf", align_bytes=64)
        q_codes = sb.tile([P, Q], U32, name="q_codes", align_bytes=64)
        q_scales = sb.tile([P, Q], U8, name="q_scales", align_bytes=64)
        interleave_cast(nc, q_bf[:], q_raw[:])
        nc.vector.quantize_mx(
            out=q_codes[:].bitcast(FP8X4), scales=q_scales[:], in_=q_bf[:].rearrange("p q t -> p (q t)")
        )

        nc.vector.tensor_copy(
            out=mixed_words[:].rearrange("p (r s) -> p s r", r=PACK), in_=words_window.indirect(offs2_t[:])
        )
        a0 = psum.tile([P, PACK, Q], F32, name="a0")
        for r in range(PACK):
            cols = slice(r * P, (r + 1) * P)
            nc.tensor.matmul_mx(
                out=a0[:, r, :],
                lhsT=mixed_words[:, cols].bitcast(FP8X4),
                lhsT_scale=mixed_scales[:, cols],
                rhs=q_codes[:].bitcast(FP8X4),
                rhs_scale=q_scales[:],
                start=True,
                stop=True,
            )

        nc.vector.tensor_copy(out=own_words[:], in_=words_window.indirect(offs_t[:]))
        scores = psum.tile([P, I], F32, name="scores")
        nc.tensor.matmul_mx(
            out=scores[:],
            lhsT=q_codes[:].bitcast(FP8X4),
            lhsT_scale=q_scales[:],
            rhs=own_words[:].bitcast(FP8X4),
            rhs_scale=own_scales[:],
            start=True,
            stop=False,
        )

        af_bf = sb.tile([P, Q, PACK], BF16, name="af_bf", align_bytes=64)
        nc.vector.tensor_tensor(
            out=af_bf[:],
            in0=a0[:].rearrange("p r q -> p q r"),
            in1=hf_t[:].unsqueeze(1).to_broadcast([P, Q, PACK]),
            op=ALU.mult,
        )

        mixer_codes = sb.tile([P, I], U32, name="mixer_codes", align_bytes=64)
        mixer_scales = sb.tile([P, I], U8, name="mixer_scales", align_bytes=64)
        af_codes = sb.tile([P, Q], U32, name="af_codes", align_bytes=64)
        af_scales = sb.tile([P, Q], U8, name="af_scales", align_bytes=64)
        for c, (raw, col, width) in enumerate(mixer_raw):
            cols = slice(col, col + width)
            grouped = sb.tile([P, width, PACK], BF16, name=f"mixer_bf{c}", align_bytes=64)
            interleave_cast(nc, grouped[:], raw[:])
            nc.vector.quantize_mx(
                out=mixer_codes[:, cols].bitcast(FP8X4),
                scales=mixer_scales[:, cols],
                in_=grouped[:].rearrange("p i t -> p (i t)"),
            )
            if c == 0:
                nc.vector.quantize_mx(
                    out=af_codes[:].bitcast(FP8X4), scales=af_scales[:], in_=af_bf[:].rearrange("p q t -> p (q t)")
                )
            nc.tensor.matmul_mx(
                out=scores[:, cols],
                lhsT=af_codes[:].bitcast(FP8X4),
                lhsT_scale=af_scales[:],
                rhs=mixer_codes[:, cols].bitcast(FP8X4),
                rhs_scale=mixer_scales[:, cols],
                start=False,
                stop=(c == len(mixer_raw) - 1),
            )

        neg_max = sb.tile([P, 1], F32, name="neg_max")
        row_sum = sb.tile([P, 1], F32, name="row_sum")
        inv_sum = sb.tile([P, 1], F32, name="inv_sum")
        nc.vector.tensor_reduce(out=neg_max[:], in_=scores[:], axis=AX.X, op=ALU.max, negate=True)
        nc.scalar.activation(
            out=p_pad[:, PAD : PAD + I], in_=scores[:], func=ACT.Exp, bias=neg_max[:], accum_out=row_sum[:]
        )
        nc.vector.reciprocal(out=inv_sum[:], in_=row_sum[:])
        rest = I - SCALAR_SLOTS
        step_s = sb.tile([P, SCALAR_SLOTS], F32, name="step_s", align_bytes=64)
        ws_s = sb.tile([P, SCALAR_SLOTS], F32, name="ws_s", align_bytes=64)
        share = sb.tile([P, rest], F32, name="share", align_bytes=64)
        pulled = sb.tile([P, rest], F32, name="pulled", align_bytes=64)
        nc.vector.scalar_tensor_tensor(
            out=step_s[:],
            in0=p_pad[:, PAD - 1 : PAD - 1 + SCALAR_SLOTS],
            scalar=neg_pull[:],
            in1=p_pad[:, PAD : PAD + SCALAR_SLOTS],
            op0=ALU.mult,
            op1=ALU.add,
        )
        first = PAD + SCALAR_SLOTS
        nc.vector.tensor_scalar(share[:], p_pad[:, first : first + rest], inv_sum[:], GAIN, ALU.mult, ALU.mult)
        nc.vector.tensor_scalar(
            pulled[:], p_pad[:, first - 1 : first - 1 + rest], inv_sum[:], pull_gain[:], ALU.mult, ALU.mult
        )
        nc.vector.tensor_scalar(ws_s[:], step_s[:], inv_sum[:], GAIN, ALU.mult, ALU.mult)
        nc.scalar.activation(
            out=placed_s[:].indirect(offs3_t[:, : SCALAR_SLOTS // 16]), in_=ws_s[:], func=ACT.Copy
        )
        nc.vector.tensor_tensor(
            out=placed_v[:].indirect(offs3_t[:, SCALAR_SLOTS // 16 :]), in0=share[:], in1=pulled[:], op=ALU.add
        )

        partial = sb.tile([P, M], F32, name="partial", align_bytes=64)

        def fade_and_add(cols):
            nc.vector.scalar_tensor_tensor(
                out=partial[:, cols],
                in0=old_t[:, cols],
                scalar=fade_t[:],
                in1=placed_v[:, cols],
                op0=ALU.mult,
                op1=ALU.add,
            )

        chunks = M // OUT_WIDTH
        fade_and_add(slice(0, EARLY_CHUNKS * OUT_WIDTH))
        for c in range(chunks):
            if EARLY_CHUNKS <= c + 1 < chunks:
                fade_and_add(slice((c + 1) * OUT_WIDTH, (c + 2) * OUT_WIDTH))
            cols = slice(c * OUT_WIDTH, (c + 1) * OUT_WIDTH)
            result = sb.tile([P, OUT_WIDTH], F32, name=f"result{c}", align_bytes=64)
            nc.vector.tensor_tensor(out=result[:], in0=partial[:, cols], in1=placed_s[:, cols], op=ALU.add)
            nc.sync.dma_start(out=out[:, cols], in_=result[:])
